import numpy as np
import ml_dtypes


def mxq(x, axis, fmt="e4m3"):
    dtype, down = {"e4m3": (ml_dtypes.float8_e4m3fn, 7), "e5m2": (ml_dtypes.float8_e5m2, 14)}[fmt]
    v = np.moveaxis(np.asarray(x, np.float32).astype(ml_dtypes.bfloat16).astype(np.float64), axis, -1)
    blocks = v.reshape(v.shape[:-1] + (-1, 32))
    amax = np.abs(blocks).max(-1, keepdims=True)
    byte = np.maximum(np.where(amax > 0, np.frexp(amax)[1] - 1 + 127, 0) - down, 1)
    scale = np.exp2(byte - 127.0)
    codes = (blocks / scale).astype(np.float32).astype(dtype).astype(np.float64)
    return np.moveaxis((codes * scale).reshape(v.shape), -1, axis)


WIDE = False


def mx_kscale(k):
    if not WIDE:
        return np.ones(k)
    levels = np.array([10, -10, 5, -5, 0])
    if k % 512:
        return np.exp2(np.random.permutation(np.resize(levels, k // 32))).repeat(32)
    a = np.empty((k // 512, 16))
    for p in range(k // 512):
        a[p, :8] = np.random.permutation(np.resize(levels, 8))
        for g in range(8):
            far = levels[np.abs(levels - a[p, g]) >= 10]
            a[p, g + 8] = far[np.random.randint(len(far))]
    return np.exp2(a.ravel()).repeat(32)


def f64(x):
    return np.asarray(x).astype(np.float64)


def striped(idx):
    return np.tile(idx.reshape(-1, 16).T, (8, 1)).astype(np.uint16)


def unstriped(offs):
    return offs[:16].T.reshape(-1).astype(np.int64)


def relu(v):
    return np.maximum(v, 0.0)


K, T, D, S, V, H, N = 512, 4096, 4, 2048, 512, 512, 512


def setup_inputs():
    n = np.random.standard_normal
    s = mx_kscale(K)[:, None]
    u = mx_kscale(H)
    return {
        "xT": (n((K, T)) * s).astype(np.float32),
        "w1": (n((K, H)) / np.sqrt(K) / s * u).astype(np.float32),
        "w2": (n((H, N)) / np.sqrt(H) / u[:, None]).astype(np.float32),
        "offs": striped(np.concatenate([np.random.permutation(T)[:V] for _ in range(D)])),
    }


def reference(xT, w1, w2, offs):
    idx = unstriped(offs)
    x = np.empty((K, V))
    for l in range(D):
        r = l // 4 * (4 * K // D) + l % 4 + 4 * np.arange(K // D)
        x[r] = f64(xT)[r][:, idx[l * V:(l + 1) * V]]
    xq = mxq(x, 0, "e4m3")
    h = relu(mxq(f64(w1), 0, "e4m3").T @ xq)
    return mxq(f64(w2), 0, "e4m3").T @ mxq(h, 0, "e4m3")

@@ -1,0 +1,159 @@
+from contextlib import ExitStack
+
+import concourse.mybir as mybir
+
+K, T, LEVELS, POINTS, H, N = 512, 4096, 4, 512, 512, 512
+P = 128
+CHUNK = 128
+FLOPS = 2 * K * H * POINTS + 2 * H * N * POINTS
+
+F32 = mybir.dt.float32
+BF16 = mybir.dt.bfloat16
+U32 = mybir.dt.uint32
+U16 = mybir.dt.uint16
+U8 = mybir.dt.uint8
+FP8X4 = mybir.dt.float8_e4m3fn_x4
+RELU = mybir.ActivationFunctionType.Relu
+MULT = mybir.AluOpType.mult
+ADD = mybir.AluOpType.add
+
+
+def tile_picked_grid_mlp_relu_sub_l_kernel(tc, xT, w1, w2, offs, out):
+    nc = tc.nc
+    with ExitStack() as ctx:
+        keep = ctx.enter_context(tc.tile_pool(name="keep", bufs=1))
+        stage = ctx.enter_context(tc.tile_pool(name="stage", bufs=4))
+        psum = ctx.enter_context(tc.psum_pool(name="psum", bufs=4))
+
+        offsets = keep.tile([P, LEVELS * POINTS // 16], U16, name="offsets")
+        w1_raw = keep.tile([P, 4, H], F32, name="w1_raw", align_bytes=64)
+        w2_raw = keep.tile([P, 4, N], F32, name="w2_raw", align_bytes=64)
+        tables = [keep.tile([P, T], F32, name=f"table{l}", align_bytes=64) for l in range(LEVELS)]
+        levels = xT.rearrange("(p j) w -> p j w", j=4)
+        nc.sync.dma_start(tables[0][:], levels[:, 0, :])
+        nc.sync.dma_start(offsets[:], offs)
+        nc.sync.dma_start(tables[1][:], levels[:, 1, :])
+        nc.sync.dma_start(tables[2][:], levels[:, 2, :])
+        nc.sync.dma_start(tables[3][:], levels[:, 3, :])
+        nc.sync.dma_start(w1_raw[:], w1.rearrange("(p j) c -> p j c", j=4))
+        nc.sync.dma_start(w2_raw[:], w2.rearrange("(p j) c -> p j c", j=4))
+
+        spark = keep.tile([P, 1], F32, name="spark")
+        nc.vector.memset(spark[:], 0.0)
+        nc.scalar.activation(spark[:], spark[:], RELU)
+
+        w1_grouped = [keep.tile([P, P, 4], BF16, name=f"w1_grouped{t}", align_bytes=64) for t in range(4)]
+        w2_grouped = [keep.tile([P, P, 4], BF16, name=f"w2_grouped{t}", align_bytes=64) for t in range(4)]
+        w1_codes = [keep.tile([P, P], U32, name=f"w1_codes{t}", align_bytes=64) for t in range(4)]
+        w1_scales = [keep.tile([P, P], U8, name=f"w1_scales{t}", align_bytes=64) for t in range(4)]
+        w2_codes = [keep.tile([P, P], U32, name=f"w2_codes{t}", align_bytes=64) for t in range(4)]
+        w2_scales = [keep.tile([P, P], U8, name=f"w2_scales{t}", align_bytes=64) for t in range(4)]
+        x = keep.tile([P, POINTS, 4], BF16, name="x", align_bytes=64)
+        x_flat = x[:].rearrange("p v j -> p (v j)")
+        x_codes = keep.tile([P, POINTS], U32, name="x_codes", align_bytes=64)
+        x_scales = keep.tile([P, POINTS], U8, name="x_scales", align_bytes=64)
+        h_banks = [psum.tile([P, 4, CHUNK], F32, name="h_bank") for c in range(4)]
+        h_codes = {}
+        out_rows = out.rearrange("(q p) v -> p q v", p=P)
+
+        def group(engine, target, source):
+            if engine == "S":
+                nc.scalar.copy(target, source)
+            elif engine == "V":
+                nc.vector.tensor_copy(out=target, in_=source)
+            else:
+                nc.gpsimd.tensor_scalar(out=target, in0=source, scalar1=1.0, scalar2=0.0, op0=MULT, op1=ADD)
+
+        def group1(engine, t):
+            group(engine, w1_grouped[t][:], w1_raw[:].rearrange("p j (m t) -> p t m j", t=4)[:, t])
+
+        def group2(engine, q):
+            group(engine, w2_grouped[q][:], w2_raw[:, :, q * P : (q + 1) * P].rearrange("p j n -> p n j"))
+
+        def quantize(codes, scales, source, a, b):
+            nc.vector.quantize_mx(
+                out=codes[:, a:b].bitcast(FP8X4), scales=scales[:, a:b], in_=source[:, 4 * a : 4 * b]
+            )
+
+        def quantize1(t):
+            quantize(w1_codes[t], w1_scales[t], w1_grouped[t][:].rearrange("p n j -> p (n j)"), 0, P)
+
+        def quantize2(q):
+            quantize(w2_codes[q], w2_scales[q], w2_grouped[q][:].rearrange("p n j -> p (n j)"), 0, P)
+
+        def quantize_x(a, b):
+            quantize(x_codes, x_scales, x_flat, a, b)
+
+        def gather(l):
+            per = POINTS // 16
+            nc.vector.tensor_copy(x[:, :, l], tables[l][:].indirect(offsets[:, l * per : (l + 1) * per]))
+
+        def product(target, w_codes, w_scales, codes, scales, cols):
+            nc.tensor.matmul_mx(
+                out=target,
+                lhsT=w_codes[:].bitcast(FP8X4),
+                lhsT_scale=w_scales[:],
+                rhs=codes[:, cols].bitcast(FP8X4),
+                rhs_scale=scales[:, cols],
+                start=True,
+                stop=True,
+            )
+
+        def warm(count):
+            for i in range(count):
+                bank = psum.tile([P, 512], F32, name="o_bank")
+                nc.tensor.matmul_mx(out=bank[:], lhsT=x_codes[:, :P].bitcast(FP8X4), lhsT_scale=x_scales[:, :P],
+                    rhs=x_codes[:].bitcast(FP8X4), rhs_scale=x_scales[:], start=True, stop=True)
+
+        def first(c, t):
+            product(h_banks[c][:, t, :], w1_codes[t], w1_scales[t], x_codes, x_scales, slice(c * CHUNK, (c + 1) * CHUNK))
+
+        def relu(engine, c):
+            h = stage.tile([P, CHUNK, 4], BF16, name="h", align_bytes=64)
+            source = h_banks[c][:].rearrange("p t n -> p n t")
+            if engine == "S":
+                nc.scalar.activation(h[:], source, RELU)
+            else:
+                nc.vector.tensor_scalar_max(h[:], source, 0.0)
+            codes = stage.tile([P, CHUNK], U32, name="h_codes", align_bytes=64)
+            scales = stage.tile([P, CHUNK], U8, name="h_scales", align_bytes=64)
+            quantize(codes, scales, h[:].rearrange("p n j -> p (n j)"), 0, CHUNK)
+            h_codes[c] = (codes, scales)
+
+        def second(engines, c):
+            codes, scales = h_codes[c]
+            result = stage.tile([P, 4, CHUNK], F32, name="result", align_bytes=64)
+            cols = slice(c * CHUNK, (c + 1) * CHUNK)
+            parts = len(engines)
+            wide = 4 // parts
+            for i in range(parts):
+                bank = psum.tile([P, wide, CHUNK], F32, name="o_bank")
+                for q in range(wide):
+                    w = wide * i + q
+                    product(bank[:, q, :], w2_codes[w], w2_scales[w], codes, scales, slice(0, CHUNK))
+                part = result[:, wide * i : wide * (i + 1), :]
+                if engines[i] == "S":
+                    nc.scalar.copy(part, bank[:])
+                else:
+                    nc.vector.tensor_copy(out=part, in_=bank[:])
+            nc.sync.dma_start(out_rows[:, :, cols], result[:])
+
+        for l in range(LEVELS):
+            gather(l)
+        quantize_x(0, 512)
+        warm(2)
+        for t, engine in enumerate("VSVS"):
+            group1(engine, t)
+        for t in (0, 2, 1, 3):
+            quantize1(t)
+        for t in (0, 2, 1, 3):
+            for c in range(4):
+                first(c, t)
+        for c in range(4):
+            relu("S", c)
+        for q, engine in enumerate("VSVV"):
+            group2(engine, q)
+        for q in (0, 2, 3, 1):
+            quantize2(q)
+        for c, engines in enumerate(("SV", "SV", "S", "VS")):
+            second(engines, c)

@@ -30,22 +30,27 @@ def tile_picked_grid_mlp_relu_sub_l_kernel(tc, xT, w1, w2, offs, out):
         w2_raw = keep.tile([P, 4, N], F32, name="w2_raw", align_bytes=64)
         tables = [keep.tile([P, T], F32, name=f"table{l}", align_bytes=64) for l in range(LEVELS)]
         levels = xT.rearrange("(p j) w -> p j w", j=4)
+
+        def load_table(l, a, b):
+            nc.sync.dma_start(tables[l][:, a:b], levels[:, l, a:b])
+
         nc.sync.dma_start(tables[0][:], levels[:, 0, :])
         nc.sync.dma_start(offsets[:], offs)
         nc.sync.dma_start(tables[1][:], levels[:, 1, :])
         nc.sync.dma_start(tables[2][:], levels[:, 2, :])
-        nc.sync.dma_start(tables[3][:], levels[:, 3, :])
+        load_table(3, 0, T // 2)
         nc.sync.dma_start(w1_raw[:], w1.rearrange("(p j) c -> p j c", j=4))
+        load_table(3, T // 2, T)
         nc.sync.dma_start(w2_raw[:], w2.rearrange("(p j) c -> p j c", j=4))
 
         spark = keep.tile([P, 1], F32, name="spark")
         nc.vector.memset(spark[:], 0.0)
         nc.scalar.activation(spark[:], spark[:], RELU)
 
-        w1_grouped = [keep.tile([P, P, 4], BF16, name=f"w1_grouped{t}", align_bytes=64) for t in range(4)]
+        w1_grouped = keep.tile([P, 4, P, 4], BF16, name="w1_grouped", align_bytes=64)
         w2_grouped = [keep.tile([P, P, 4], BF16, name=f"w2_grouped{t}", align_bytes=64) for t in range(4)]
-        w1_codes = [keep.tile([P, P], U32, name=f"w1_codes{t}", align_bytes=64) for t in range(4)]
-        w1_scales = [keep.tile([P, P], U8, name=f"w1_scales{t}", align_bytes=64) for t in range(4)]
+        w1_codes = keep.tile([P, 4 * P], U32, name="w1_codes", align_bytes=64)
+        w1_scales = keep.tile([P, 4 * P], U8, name="w1_scales", align_bytes=64)
         w2_codes = [keep.tile([P, P], U32, name=f"w2_codes{t}", align_bytes=64) for t in range(4)]
         w2_scales = [keep.tile([P, P], U8, name=f"w2_scales{t}", align_bytes=64) for t in range(4)]
         x = keep.tile([P, POINTS, 4], BF16, name="x", align_bytes=64)
@@ -64,19 +69,19 @@ def tile_picked_grid_mlp_relu_sub_l_kernel(tc, xT, w1, w2, offs, out):
             else:
                 nc.gpsimd.tensor_scalar(out=target, in0=source, scalar1=1.0, scalar2=0.0, op0=MULT, op1=ADD)
 
-        def group1(engine, t):
-            group(engine, w1_grouped[t][:], w1_raw[:].rearrange("p j (m t) -> p t m j", t=4)[:, t])
+        def group1(engine, a, b):
+            group(engine, w1_grouped[:, :, a:b, :].rearrange("p t m j -> p m j t"), w1_raw[:].rearrange("p j (m t) -> p m j t", t=4)[:, a:b])
 
         def group2(engine, q):
-            group(engine, w2_grouped[q][:], w2_raw[:, :, q * P : (q + 1) * P].rearrange("p j n -> p n j"))
+            group(engine, w2_grouped[q][:].rearrange("p (c i) j -> p c j i", i=4), w2_raw[:, :, q * P : (q + 1) * P].rearrange("p j (c i) -> p c j i", i=4))
 
         def quantize(codes, scales, source, a, b):
             nc.vector.quantize_mx(
                 out=codes[:, a:b].bitcast(FP8X4), scales=scales[:, a:b], in_=source[:, 4 * a : 4 * b]
             )
 
-        def quantize1(t):
-            quantize(w1_codes[t], w1_scales[t], w1_grouped[t][:].rearrange("p n j -> p (n j)"), 0, P)
+        def quantize1(a, b):
+            quantize(w1_codes, w1_scales, w1_grouped[:].rearrange("p t m j -> p (t m j)"), a * P, b * P)
 
         def quantize2(q):
             quantize(w2_codes[q], w2_scales[q], w2_grouped[q][:].rearrange("p n j -> p (n j)"), 0, P)
@@ -91,8 +96,8 @@ def tile_picked_grid_mlp_relu_sub_l_kernel(tc, xT, w1, w2, offs, out):
         def product(target, w_codes, w_scales, codes, scales, cols):
             nc.tensor.matmul_mx(
                 out=target,
-                lhsT=w_codes[:].bitcast(FP8X4),
-                lhsT_scale=w_scales[:],
+                lhsT=w_codes.bitcast(FP8X4),
+                lhsT_scale=w_scales,
                 rhs=codes[:, cols].bitcast(FP8X4),
                 rhs_scale=scales[:, cols],
                 start=True,
@@ -102,11 +107,11 @@ def tile_picked_grid_mlp_relu_sub_l_kernel(tc, xT, w1, w2, offs, out):
         def warm(count):
             for i in range(count):
                 bank = psum.tile([P, 512], F32, name="o_bank")
-                nc.tensor.matmul_mx(out=bank[:], lhsT=x_codes[:, :P].bitcast(FP8X4), lhsT_scale=x_scales[:, :P],
-                    rhs=x_codes[:].bitcast(FP8X4), rhs_scale=x_scales[:], start=True, stop=True)
+                nc.tensor.matmul_mx(out=bank[:], lhsT=w1_codes[:, :P].bitcast(FP8X4), lhsT_scale=w1_scales[:, :P],
+                    rhs=w1_codes[:].bitcast(FP8X4), rhs_scale=w1_scales[:], start=True, stop=True)
 
         def first(c, t):
-            product(h_banks[c][:, t, :], w1_codes[t], w1_scales[t], x_codes, x_scales, slice(c * CHUNK, (c + 1) * CHUNK))
+            product(h_banks[c][:, t, :], w1_codes[:, t * P : (t + 1) * P], w1_scales[:, t * P : (t + 1) * P], x_codes, x_scales, slice(c * CHUNK, (c + 1) * CHUNK))
 
         def relu(engine, c):
             h = stage.tile([P, CHUNK, 4], BF16, name="h", align_bytes=64)
@@ -130,7 +135,7 @@ def tile_picked_grid_mlp_relu_sub_l_kernel(tc, xT, w1, w2, offs, out):
                 bank = psum.tile([P, wide, CHUNK], F32, name="o_bank")
                 for q in range(wide):
                     w = wide * i + q
-                    product(bank[:, q, :], w2_codes[w], w2_scales[w], codes, scales, slice(0, CHUNK))
+                    product(bank[:, q, :], w2_codes[w][:], w2_scales[w][:], codes, scales, slice(0, CHUNK))
                 part = result[:, wide * i : wide * (i + 1), :]
                 if engines[i] == "S":
                     nc.scalar.copy(part, bank[:])
@@ -138,22 +143,24 @@ def tile_picked_grid_mlp_relu_sub_l_kernel(tc, xT, w1, w2, offs, out):
                     nc.vector.tensor_copy(out=part, in_=bank[:])
             nc.sync.dma_start(out_rows[:, :, cols], result[:])
 
-        for l in range(LEVELS):
+        for l in range(3):
             gather(l)
-        quantize_x(0, 512)
+        group1("V", 0, 88)
+        group1("S", 88, 128)
+        quantize1(0, 4)
         warm(2)
-        for t, engine in enumerate("VSVS"):
-            group1(engine, t)
-        for t in (0, 2, 1, 3):
-            quantize1(t)
-        for t in (0, 2, 1, 3):
-            for c in range(4):
-                first(c, t)
+        gather(3)
+        quantize_x(0, 128)
+        quantize_x(128, 256)
+        quantize_x(256, 512)
         for c in range(4):
-            relu("S", c)
-        for q, engine in enumerate("VSVV"):
+            for t in range(4):
+                first(c, t)
+        for q, engine in enumerate("VSVS"):
             group2(engine, q)
-        for q in (0, 2, 3, 1):
+        for c, engine in enumerate("VSSS"):
+            relu(engine, c)
+        for q in range(4):
             quantize2(q)
-        for c, engines in enumerate(("SV", "SV", "S", "VS")):
+        for c, engines in enumerate(("S", "SV", "VS", "VS")):
             second(engines, c)

@@ -23,7 +23,7 @@ def tile_picked_grid_mlp_relu_sub_l_kernel(tc, xT, w1, w2, offs, out):
     with ExitStack() as ctx:
         keep = ctx.enter_context(tc.tile_pool(name="keep", bufs=1))
         stage = ctx.enter_context(tc.tile_pool(name="stage", bufs=4))
-        psum = ctx.enter_context(tc.psum_pool(name="psum", bufs=4))
+        psum = ctx.enter_context(tc.psum_pool(name="psum", bufs=8))
 
         offsets = keep.tile([P, LEVELS * POINTS // 16], U16, name="offsets")
         w1_raw = keep.tile([P, 4, H], F32, name="w1_raw", align_bytes=64)
@@ -31,37 +31,37 @@ def tile_picked_grid_mlp_relu_sub_l_kernel(tc, xT, w1, w2, offs, out):
         tables = [keep.tile([P, T], F32, name=f"table{l}", align_bytes=64) for l in range(LEVELS)]
         levels = xT.rearrange("(p j) w -> p j w", j=4)
 
-        def load_table(l, a, b):
+        def load_table(l, a=0, b=T):
             nc.sync.dma_start(tables[l][:, a:b], levels[:, l, a:b])
 
-        nc.sync.dma_start(tables[0][:], levels[:, 0, :])
+        load_table(0)
         nc.sync.dma_start(offsets[:], offs)
-        nc.sync.dma_start(tables[1][:], levels[:, 1, :])
-        nc.sync.dma_start(tables[2][:], levels[:, 2, :])
+        load_table(1)
+        load_table(2)
         load_table(3, 0, T // 2)
         nc.sync.dma_start(w1_raw[:], w1.rearrange("(p j) c -> p j c", j=4))
         load_table(3, T // 2, T)
         nc.sync.dma_start(w2_raw[:], w2.rearrange("(p j) c -> p j c", j=4))
 
+        ones = keep.tile([P, CHUNK], F32, name="ones", align_bytes=64)
         spark = keep.tile([P, 1], F32, name="spark")
-        nc.vector.memset(spark[:], 0.0)
-        nc.scalar.activation(spark[:], spark[:], RELU)
+        nc.vector.memset(ones[:], 1.0)
+        nc.scalar.activation(spark[:], ones[:, :1], RELU)
 
         w1_grouped = keep.tile([P, 4, P, 4], BF16, name="w1_grouped", align_bytes=64)
-        w2_grouped = [keep.tile([P, P, 4], BF16, name=f"w2_grouped{t}", align_bytes=64) for t in range(4)]
-        w1_codes = keep.tile([P, 4 * P], U32, name="w1_codes", align_bytes=64)
-        w1_scales = keep.tile([P, 4 * P], U8, name="w1_scales", align_bytes=64)
-        w2_codes = [keep.tile([P, P], U32, name=f"w2_codes{t}", align_bytes=64) for t in range(4)]
-        w2_scales = [keep.tile([P, P], U8, name=f"w2_scales{t}", align_bytes=64) for t in range(4)]
+        w1_codes = keep.tile([P, H], U32, name="w1_codes", align_bytes=64)
+        w1_scales = keep.tile([P, H], U8, name="w1_scales", align_bytes=64)
+        w2_grouped = keep.tile([P, N, 4], BF16, name="w2_grouped", align_bytes=64)
+        w2_codes = [keep.tile([P, N // 2], U32, name=f"w2_codes{i}", align_bytes=64) for i in range(2)]
+        w2_scales = [keep.tile([P, N // 2], U8, name=f"w2_scales{i}", align_bytes=64) for i in range(2)]
+        picked = keep.tile([P, 2, POINTS], F32, name="picked", align_bytes=64)
         x = keep.tile([P, POINTS, 4], BF16, name="x", align_bytes=64)
-        x_flat = x[:].rearrange("p v j -> p (v j)")
         x_codes = keep.tile([P, POINTS], U32, name="x_codes", align_bytes=64)
         x_scales = keep.tile([P, POINTS], U8, name="x_scales", align_bytes=64)
-        h_banks = [psum.tile([P, 4, CHUNK], F32, name="h_bank") for c in range(4)]
-        h_codes = {}
+        h_banks, h_codes = {}, {}
         out_rows = out.rearrange("(q p) v -> p q v", p=P)
 
-        def group(engine, target, source):
+        def copy(engine, target, source):
             if engine == "S":
                 nc.scalar.copy(target, source)
             elif engine == "V":
@@ -70,48 +70,75 @@ def tile_picked_grid_mlp_relu_sub_l_kernel(tc, xT, w1, w2, offs, out):
                 nc.gpsimd.tensor_scalar(out=target, in0=source, scalar1=1.0, scalar2=0.0, op0=MULT, op1=ADD)
 
         def group1(engine, a, b):
-            group(engine, w1_grouped[:, :, a:b, :].rearrange("p t m j -> p m j t"), w1_raw[:].rearrange("p j (m t) -> p m j t", t=4)[:, a:b])
-
-        def group2(engine, q):
-            group(engine, w2_grouped[q][:].rearrange("p (c i) j -> p c j i", i=4), w2_raw[:, :, q * P : (q + 1) * P].rearrange("p j (c i) -> p c j i", i=4))
-
-        def quantize(codes, scales, source, a, b):
-            nc.vector.quantize_mx(
-                out=codes[:, a:b].bitcast(FP8X4), scales=scales[:, a:b], in_=source[:, 4 * a : 4 * b]
+            copy(
+                engine,
+                w1_grouped[:, :, a:b, :].rearrange("p t m j -> p m j t"),
+                w1_raw[:].rearrange("p j (m t) -> p m j t", t=4)[:, a:b],
             )
 
-        def quantize1(a, b):
-            quantize(w1_codes, w1_scales, w1_grouped[:].rearrange("p t m j -> p (t m j)"), a * P, b * P)
+        def group2(engine, q, parts=4):
+            a, b = q * N // parts, (q + 1) * N // parts
+            copy(
+                engine,
+                w2_grouped[:, a:b, :].rearrange("p (c i) j -> p c j i", i=4),
+                w2_raw[:, :, a:b].rearrange("p j (c i) -> p c j i", i=4),
+            )
 
-        def quantize2(q):
-            quantize(w2_codes[q], w2_scales[q], w2_grouped[q][:].rearrange("p n j -> p (n j)"), 0, P)
+        def quantize(codes, scales, source):
+            nc.vector.quantize_mx(out=codes.bitcast(FP8X4), scales=scales, in_=source.rearrange("p n j -> p (n j)"))
+
+        def quantize1():
+            quantize(w1_codes[:], w1_scales[:], w1_grouped[:].rearrange("p t m j -> p (t m) j"))
+
+        def quantize2(a, b):
+            n = N // 4
+            i = a // 2
+            quantize(w2_codes[i][:, (a % 2) * n : (b - 2 * i) * n], w2_scales[i][:, (a % 2) * n : (b - 2 * i) * n], w2_grouped[:, a * n : b * n, :])
 
         def quantize_x(a, b):
-            quantize(x_codes, x_scales, x_flat, a, b)
+            quantize(x_codes[:, a:b], x_scales[:, a:b], x[:, a:b, :])
+
+        per = POINTS // 16
 
         def gather(l):
-            per = POINTS // 16
-            nc.vector.tensor_copy(x[:, :, l], tables[l][:].indirect(offsets[:, l * per : (l + 1) * per]))
+            target = x[:, :, l] if l < 2 else picked[:, l - 2, :]
+            nc.vector.tensor_copy(target, tables[l][:].indirect(offsets[:, l * per : (l + 1) * per]))
 
-        def product(target, w_codes, w_scales, codes, scales, cols):
+        def gather_last(c):
+            first_column = 3 * per + c * CHUNK // 16
+            nc.vector.tensor_tensor(
+                picked[:, 1, c * CHUNK : (c + 1) * CHUNK],
+                tables[3][:].indirect(offsets[:, first_column : first_column + CHUNK // 16]),
+                ones[:],
+                MULT,
+            )
+
+        def pair(c, engine):
+            cols = slice(c * CHUNK, (c + 1) * CHUNK)
+            copy(engine, x[:, cols, 2:4], picked[:, :, cols].rearrange("p l n -> p n l"))
+
+        def product(target, w_codes, w_scales, codes, scales):
             nc.tensor.matmul_mx(
                 out=target,
                 lhsT=w_codes.bitcast(FP8X4),
                 lhsT_scale=w_scales,
-                rhs=codes[:, cols].bitcast(FP8X4),
-                rhs_scale=scales[:, cols],
+                rhs=codes.bitcast(FP8X4),
+                rhs_scale=scales,
                 start=True,
                 stop=True,
             )
 
         def warm(count):
             for i in range(count):
-                bank = psum.tile([P, 512], F32, name="o_bank")
-                nc.tensor.matmul_mx(out=bank[:], lhsT=w1_codes[:, :P].bitcast(FP8X4), lhsT_scale=w1_scales[:, :P],
-                    rhs=w1_codes[:].bitcast(FP8X4), rhs_scale=w1_scales[:], start=True, stop=True)
+                bank = psum.tile([P, H], F32, name="bank")
+                product(bank[:], w1_codes[:, :P], w1_scales[:, :P], w1_codes[:], w1_scales[:])
 
         def first(c, t):
-            product(h_banks[c][:, t, :], w1_codes[:, t * P : (t + 1) * P], w1_scales[:, t * P : (t + 1) * P], x_codes, x_scales, slice(c * CHUNK, (c + 1) * CHUNK))
+            if t == 0:
+                bank = psum.tile([P, 4, CHUNK], F32, name="bank")
+                h_banks[c] = bank
+            rows, cols = slice(t * P, (t + 1) * P), slice(c * CHUNK, (c + 1) * CHUNK)
+            product(h_banks[c][:, t, :], w1_codes[:, rows], w1_scales[:, rows], x_codes[:, cols], x_scales[:, cols])
 
         def relu(engine, c):
             h = stage.tile([P, CHUNK, 4], BF16, name="h", align_bytes=64)
@@ -122,45 +149,41 @@ def tile_picked_grid_mlp_relu_sub_l_kernel(tc, xT, w1, w2, offs, out):
                 nc.vector.tensor_scalar_max(h[:], source, 0.0)
             codes = stage.tile([P, CHUNK], U32, name="h_codes", align_bytes=64)
             scales = stage.tile([P, CHUNK], U8, name="h_scales", align_bytes=64)
-            quantize(codes, scales, h[:].rearrange("p n j -> p (n j)"), 0, CHUNK)
+            quantize(codes[:], scales[:], h[:])
             h_codes[c] = (codes, scales)
 
         def second(engines, c):
             codes, scales = h_codes[c]
-            result = stage.tile([P, 4, CHUNK], F32, name="result", align_bytes=64)
-            cols = slice(c * CHUNK, (c + 1) * CHUNK)
-            parts = len(engines)
-            wide = 4 // parts
-            for i in range(parts):
-                bank = psum.tile([P, wide, CHUNK], F32, name="o_bank")
+            wide = 4 // len(engines)
+            for i, engine in enumerate(engines):
+                bank = psum.tile([P, wide, CHUNK], F32, name="bank")
                 for q in range(wide):
                     w = wide * i + q
-                    product(bank[:, q, :], w2_codes[w][:], w2_scales[w][:], codes, scales, slice(0, CHUNK))
-                part = result[:, wide * i : wide * (i + 1), :]
-                if engines[i] == "S":
-                    nc.scalar.copy(part, bank[:])
-                else:
-                    nc.vector.tensor_copy(out=part, in_=bank[:])
-            nc.sync.dma_start(out_rows[:, :, cols], result[:])
+                    cols = slice((w % 2) * P, (w % 2 + 1) * P)
+                    product(bank[:, q, :], w2_codes[w // 2][:, cols], w2_scales[w // 2][:, cols], codes[:], scales[:])
+                result = stage.tile([P, wide, CHUNK], F32, name="result", bufs=8, align_bytes=64)
+                copy(engine, result[:], bank[:])
+                nc.sync.dma_start(out_rows[:, wide * i : wide * (i + 1), c * CHUNK : (c + 1) * CHUNK], result[:])
 
         for l in range(3):
             gather(l)
         group1("V", 0, 88)
         group1("S", 88, 128)
-        quantize1(0, 4)
+        quantize1()
         warm(2)
-        gather(3)
-        quantize_x(0, 128)
-        quantize_x(128, 256)
-        quantize_x(256, 512)
+        for c in range(4):
+            gather_last(c)
+            pair(c, "SVSS"[c])
+        for c in range(4):
+            quantize_x(c * CHUNK, (c + 1) * CHUNK)
         for c in range(4):
             for t in range(4):
                 first(c, t)
-        for q, engine in enumerate("VSVS"):
-            group2(engine, q)
-        for c, engine in enumerate("VSSS"):
-            relu(engine, c)
         for q in range(4):
-            quantize2(q)
-        for c, engines in enumerate(("S", "SV", "VS", "VS")):
-            second(engines, c)
+            group2("VSVV"[q], q)
+        for c in range(4):
+            relu("SSSS"[c], c)
+        quantize2(0, 2)
+        quantize2(2, 4)
+        for c in range(4):
+            second(["SV","VS","SV","VS"][c], c)

from contextlib import ExitStack

import concourse.mybir as mybir

K, T, LEVELS, POINTS, H, N = 512, 4096, 4, 512, 512, 512
P = 128
CHUNK = 128
FLOPS = 2 * K * H * POINTS + 2 * H * N * POINTS

F32 = mybir.dt.float32
BF16 = mybir.dt.bfloat16
U32 = mybir.dt.uint32
U16 = mybir.dt.uint16
U8 = mybir.dt.uint8
FP8X4 = mybir.dt.float8_e4m3fn_x4
RELU = mybir.ActivationFunctionType.Relu
MULT = mybir.AluOpType.mult
ADD = mybir.AluOpType.add


def tile_picked_grid_mlp_relu_sub_l_kernel(tc, xT, w1, w2, offs, out):
    nc = tc.nc
    with ExitStack() as ctx:
        keep = ctx.enter_context(tc.tile_pool(name="keep", bufs=1))
        stage = ctx.enter_context(tc.tile_pool(name="stage", bufs=4))
        psum = ctx.enter_context(tc.psum_pool(name="psum", bufs=8))

        offsets = keep.tile([P, LEVELS * POINTS // 16], U16, name="offsets")
        w1_raw = keep.tile([P, 4, H], F32, name="w1_raw", align_bytes=64)
        w2_raw = keep.tile([P, 4, N], F32, name="w2_raw", align_bytes=64)
        tables = [keep.tile([P, T], F32, name=f"table{l}", align_bytes=64) for l in range(LEVELS)]
        levels = xT.rearrange("(p j) w -> p j w", j=4)

        def load_table(l, a=0, b=T):
            nc.sync.dma_start(tables[l][:, a:b], levels[:, l, a:b])

        load_table(0)
        nc.sync.dma_start(offsets[:], offs)
        load_table(1)
        load_table(2)
        load_table(3, 0, T // 2)
        nc.sync.dma_start(w1_raw[:], w1.rearrange("(p j) c -> p j c", j=4))
        load_table(3, T // 2, T)
        nc.sync.dma_start(w2_raw[:], w2.rearrange("(p j) c -> p j c", j=4))

        ones = keep.tile([P, CHUNK], F32, name="ones", align_bytes=64)
        spark = keep.tile([P, 1], F32, name="spark")
        nc.vector.memset(ones[:], 1.0)
        nc.scalar.activation(spark[:], ones[:, :1], RELU)

        w1_grouped = keep.tile([P, 4, P, 4], BF16, name="w1_grouped", align_bytes=64)
        w1_codes = keep.tile([P, H], U32, name="w1_codes", align_bytes=64)
        w1_scales = keep.tile([P, H], U8, name="w1_scales", align_bytes=64)
        w2_grouped = keep.tile([P, N, 4], BF16, name="w2_grouped", align_bytes=64)
        w2_codes = [keep.tile([P, N // 2], U32, name=f"w2_codes{i}", align_bytes=64) for i in range(2)]
        w2_scales = [keep.tile([P, N // 2], U8, name=f"w2_scales{i}", align_bytes=64) for i in range(2)]
        picked = keep.tile([P, 2, POINTS], F32, name="picked", align_bytes=64)
        x = keep.tile([P, POINTS, 4], BF16, name="x", align_bytes=64)
        x_codes = keep.tile([P, POINTS], U32, name="x_codes", align_bytes=64)
        x_scales = keep.tile([P, POINTS], U8, name="x_scales", align_bytes=64)
        h_banks, h_codes = {}, {}
        out_rows = out.rearrange("(q p) v -> p q v", p=P)

        def copy(engine, target, source):
            if engine == "S":
                nc.scalar.copy(target, source)
            elif engine == "V":
                nc.vector.tensor_copy(out=target, in_=source)
            else:
                nc.gpsimd.tensor_scalar(out=target, in0=source, scalar1=1.0, scalar2=0.0, op0=MULT, op1=ADD)

        def group1(engine, a, b):
            copy(
                engine,
                w1_grouped[:, :, a:b, :].rearrange("p t m j -> p m j t"),
                w1_raw[:].rearrange("p j (m t) -> p m j t", t=4)[:, a:b],
            )

        def group2(engine, q, parts=4):
            a, b = q * N // parts, (q + 1) * N // parts
            copy(
                engine,
                w2_grouped[:, a:b, :].rearrange("p (c i) j -> p c j i", i=4),
                w2_raw[:, :, a:b].rearrange("p j (c i) -> p c j i", i=4),
            )

        def quantize(codes, scales, source):
            nc.vector.quantize_mx(out=codes.bitcast(FP8X4), scales=scales, in_=source.rearrange("p n j -> p (n j)"))

        def quantize1():
            quantize(w1_codes[:], w1_scales[:], w1_grouped[:].rearrange("p t m j -> p (t m) j"))

        def quantize2(a, b):
            n = N // 4
            i = a // 2
            quantize(w2_codes[i][:, (a % 2) * n : (b - 2 * i) * n], w2_scales[i][:, (a % 2) * n : (b - 2 * i) * n], w2_grouped[:, a * n : b * n, :])

        def quantize_x(a, b):
            quantize(x_codes[:, a:b], x_scales[:, a:b], x[:, a:b, :])

        per = POINTS // 16

        def gather(l):
            target = x[:, :, l] if l < 2 else picked[:, l - 2, :]
            nc.vector.tensor_copy(target, tables[l][:].indirect(offsets[:, l * per : (l + 1) * per]))

        def gather_last(c):
            first_column = 3 * per + c * CHUNK // 16
            nc.vector.tensor_tensor(
                picked[:, 1, c * CHUNK : (c + 1) * CHUNK],
                tables[3][:].indirect(offsets[:, first_column : first_column + CHUNK // 16]),
                ones[:],
                MULT,
            )

        def pair(c, engine):
            cols = slice(c * CHUNK, (c + 1) * CHUNK)
            copy(engine, x[:, cols, 2:4], picked[:, :, cols].rearrange("p l n -> p n l"))

        def product(target, w_codes, w_scales, codes, scales):
            nc.tensor.matmul_mx(
                out=target,
                lhsT=w_codes.bitcast(FP8X4),
                lhsT_scale=w_scales,
                rhs=codes.bitcast(FP8X4),
                rhs_scale=scales,
                start=True,
                stop=True,
            )

        def warm(count):
            for i in range(count):
                bank = psum.tile([P, H], F32, name="bank")
                product(bank[:], w1_codes[:, :P], w1_scales[:, :P], w1_codes[:], w1_scales[:])

        def first(c, t):
            if t == 0:
                bank = psum.tile([P, 4, CHUNK], F32, name="bank")
                h_banks[c] = bank
            rows, cols = slice(t * P, (t + 1) * P), slice(c * CHUNK, (c + 1) * CHUNK)
            product(h_banks[c][:, t, :], w1_codes[:, rows], w1_scales[:, rows], x_codes[:, cols], x_scales[:, cols])

        def relu(engine, c):
            h = stage.tile([P, CHUNK, 4], BF16, name="h", align_bytes=64)
            source = h_banks[c][:].rearrange("p t n -> p n t")
            if engine == "S":
                nc.scalar.activation(h[:], source, RELU)
            else:
                nc.vector.tensor_scalar_max(h[:], source, 0.0)
            codes = stage.tile([P, CHUNK], U32, name="h_codes", align_bytes=64)
            scales = stage.tile([P, CHUNK], U8, name="h_scales", align_bytes=64)
            quantize(codes[:], scales[:], h[:])
            h_codes[c] = (codes, scales)

        def second(engines, c):
            codes, scales = h_codes[c]
            wide = 4 // len(engines)
            for i, engine in enumerate(engines):
                bank = psum.tile([P, wide, CHUNK], F32, name="bank")
                for q in range(wide):
                    w = wide * i + q
                    cols = slice((w % 2) * P, (w % 2 + 1) * P)
                    product(bank[:, q, :], w2_codes[w // 2][:, cols], w2_scales[w // 2][:, cols], codes[:], scales[:])
                result = stage.tile([P, wide, CHUNK], F32, name="result", bufs=8, align_bytes=64)
                copy(engine, result[:], bank[:])
                nc.sync.dma_start(out_rows[:, wide * i : wide * (i + 1), c * CHUNK : (c + 1) * CHUNK], result[:])

        for l in range(3):
            gather(l)
        group1("V", 0, 88)
        group1("S", 88, 128)
        quantize1()
        warm(2)
        for c in range(4):
            gather_last(c)
            pair(c, "SVSS"[c])
        for c in range(4):
            quantize_x(c * CHUNK, (c + 1) * CHUNK)
        for c in range(4):
            for t in range(4):
                first(c, t)
        for q in range(4):
            group2("VSVV"[q], q)
        for c in range(4):
            relu("SSSS"[c], c)
        quantize2(0, 2)
        quantize2(2, 4)
        for c in range(4):
            second(["SV","VS","SV","VS"][c], c)
